import numpy as np
import ml_dtypes


def mxq(x, axis, fmt="e4m3"):
    dtype, down = {"e4m3": (ml_dtypes.float8_e4m3fn, 7), "e5m2": (ml_dtypes.float8_e5m2, 14)}[fmt]
    v = np.moveaxis(np.asarray(x, np.float32).astype(ml_dtypes.bfloat16).astype(np.float64), axis, -1)
    blocks = v.reshape(v.shape[:-1] + (-1, 32))
    amax = np.abs(blocks).max(-1, keepdims=True)
    byte = np.maximum(np.where(amax > 0, np.frexp(amax)[1] - 1 + 127, 0) - down, 1)
    scale = np.exp2(byte - 127.0)
    codes = (blocks / scale).astype(np.float32).astype(dtype).astype(np.float64)
    return np.moveaxis((codes * scale).reshape(v.shape), -1, axis)


WIDE = False


def mx_kscale(k):
    if not WIDE:
        return np.ones(k)
    levels = np.array([10, -10, 5, -5, 0])
    if k % 512:
        return np.exp2(np.random.permutation(np.resize(levels, k // 32))).repeat(32)
    a = np.empty((k // 512, 16))
    for p in range(k // 512):
        a[p, :8] = np.random.permutation(np.resize(levels, 8))
        for g in range(8):
            far = levels[np.abs(levels - a[p, g]) >= 10]
            a[p, g + 8] = far[np.random.randint(len(far))]
    return np.exp2(a.ravel()).repeat(32)


def f64(x):
    return np.asarray(x).astype(np.float64)


def striped(idx):
    return np.tile(idx.reshape(-1, 16).T, (8, 1)).astype(np.uint16)


def unstriped(offs):
    return offs[:16].T.reshape(-1).astype(np.int64)


def striped8(idx):
    return np.concatenate([x.reshape(-1, 16).T for x in idx]).astype(np.uint16)


def runs(offs, k):
    lists = np.stack([offs[16 * r : 16 * r + 16].T.reshape(-1) for r in range(8)]).astype(np.int64)
    return lists[np.arange(k) % 512 // 64]


def pack_weight(w):
    k, n = w.shape
    w = f64(np.asarray(w, np.float32).astype(ml_dtypes.bfloat16)).reshape(k // 32, 32, n)
    amax = np.abs(w).max(1)
    byte = np.clip(np.where(amax > 0, np.frexp(amax)[1] - 1 + 127 - 7, 1), 1, 254)
    scaled = (w * np.exp2(127.0 - byte)[:, None, :]).reshape(k, n).astype(np.float32)
    words = np.ascontiguousarray(scaled.reshape(k // 512, 128, 4, n).transpose(0, 1, 3, 2)).astype(ml_dtypes.float8_e4m3fn).view(np.uint8)
    return words, np.ascontiguousarray(byte.astype(np.uint8).reshape(k // 512, 16, n))


def unpack_weight(words, scales):
    g, p, n, _ = words.shape
    vals = np.ascontiguousarray(words).view(ml_dtypes.float8_e4m3fn).astype(np.float64) * np.repeat(np.exp2(scales.astype(np.float64) - 127.0), 8, axis=1)[..., None]
    return vals.transpose(0, 1, 3, 2).reshape(g * 512, n)

def planes(y):
    n, m = y.shape
    v = y.astype(np.float32).astype(ml_dtypes.bfloat16).astype(np.float64).reshape(n // 32, 32, m)
    top = np.abs(v).max(1)
    byte = np.clip(np.where(top > 0, np.frexp(top)[1] - 1 + 127 - 7, 1), 1, 254)
    codes = (v * np.exp2(127.0 - byte)[:, None, :]).reshape(n, m).astype(np.float32).astype(ml_dtypes.float8_e4m3fn).view(np.uint8)
    words = codes.reshape(n // 512, 128, 4, m).transpose(0, 1, 3, 2)
    return np.ascontiguousarray(words), np.ascontiguousarray(byte.astype(np.uint8).reshape(n // 512, 16, m))


K, T, S, N, G, H, U = 512, 1024, 512, 512, 2048, 512, 1024


def setup_inputs():
    n = np.random.standard_normal
    s = mx_kscale(K)[:, None]
    u = mx_kscale(S)
    packed_xT = pack_weight(n((K, T)) * s)
    packed_dT = pack_weight(n((K, G)) / s)
    packed_w1 = pack_weight(n((H, N)) / np.sqrt(H) / u[:, None])
    return {
        "x_words": packed_xT[0],
        "x_scales": packed_xT[1],
        "d_words": packed_dT[0],
        "d_scales": packed_dT[1],
        "gn": (np.random.uniform(0.5, 1.5, (H, 1)) * u[:, None]).astype(np.float32),
        "w1_words": packed_w1[0],
        "w1_scales": packed_w1[1],
        "mem": n((N, U)).astype(np.float32),
        "offs": striped(np.random.permutation(T)[:S]),
        "k1": striped8(np.random.randint(0, G, (8, H))),
        "two": striped(np.random.permutation(T)[:S]),
        "k2": striped8(np.random.randint(0, G, (8, H))),
        "n1": striped8(np.stack([np.random.permutation(S) for _ in range(8)])),
        "n2": striped8(np.stack([np.random.permutation(S) for _ in range(8)])),
        "n3": striped8(np.stack([np.random.permutation(S) for _ in range(8)])),
        "n4": striped8(np.stack([np.random.permutation(S) for _ in range(8)])),
        "n5": striped(np.random.permutation(U)[:S]),
    }


def reference(x_words, x_scales, d_words, d_scales, gn, w1_words, w1_scales, mem, offs, k1, two, k2, n1, n2, n3, n4, n5):
    d_k1 = unpack_weight(d_words, d_scales)[np.arange(K)[:, None], runs(k1, K)]
    xq = unpack_weight(x_words, x_scales)[:, unstriped(offs)]
    a = 0.0625 * (d_k1.T @ xq)
    d_k2 = unpack_weight(d_words, d_scales)[np.arange(K)[:, None], runs(k2, K)]
    x_two = unpack_weight(x_words, x_scales)[:, unstriped(two)]
    b = 0.0625 * (d_k2.T @ x_two)
    z = f64(gn) * (np.maximum(a[np.arange(H)[:, None], runs(n1, H)] + b[np.arange(H)[:, None], runs(n3, H)], a[np.arange(H)[:, None], runs(n2, H)] + b[np.arange(H)[:, None], runs(n4, H)]))
    h = unpack_weight(w1_words, w1_scales).T @ mxq(z, 0, "e4m3")
    nw = np.maximum(h, 0.5 * f64(mem)[:, unstriped(n5)])
    out = f64(mem).copy()
    out[:, unstriped(n5)] = nw
    return (out,) + planes(out)

@@ -1,0 +1,193 @@
+from contextlib import ExitStack
+
+import concourse.mybir as mybir
+
+K, T, S, N, G, H, U = 512, 1024, 512, 512, 2048, 512, 1024
+FLOPS = 2 * K * H * S * 2 + 2 * H * N * S
+
+F32 = mybir.dt.float32
+BF16 = mybir.dt.bfloat16
+I32 = mybir.dt.int32
+U32 = mybir.dt.uint32
+U16 = mybir.dt.uint16
+U8 = mybir.dt.uint8
+FP8X4 = mybir.dt.float8_e4m3fn_x4
+ADD = mybir.AluOpType.add
+MULT = mybir.AluOpType.mult
+MAX = mybir.AluOpType.max
+COPY = mybir.ActivationFunctionType.Copy
+
+P = 128
+PACK = 4
+HALF = S // 2
+HALF_COLS = HALF // 16
+OUT_PARTS = 4
+OUT_W = U // OUT_PARTS
+
+
+def words_of(dram):
+    return dram[0].rearrange("p n t -> p (n t)").bitcast(I32)
+
+
+def tile_picked_twpqpathbpagex_none_po_kernel(
+    tc, x_words, x_scales, d_words, d_scales, gn, w1_words, w1_scales, mem,
+    offs, k1, two, k2, n1, n2, n3, n4, n5, out_0, out_1, out_2,
+):
+    nc = tc.nc
+    with ExitStack() as ctx:
+        keep = ctx.enter_context(tc.tile_pool(name="keep", bufs=1))
+        ring = ctx.enter_context(tc.tile_pool(name="ring", bufs=3))
+        psum = ctx.enter_context(tc.psum_pool(name="psum", bufs=1))
+
+        def load_list(name, dram):
+            tile = keep.tile([P, S // 16], U16, name=name)
+            nc.sync.dma_start(tile[:], dram)
+            return tile
+
+        d_sc = keep.tile([P, G], U8, name="d_sc")
+        x_sc = keep.tile([P, T], U8, name="x_sc")
+        gain_raw = keep.tile([P, PACK], F32, name="gain_raw")
+        nc.scalar.dma_start(d_sc[:].bitcast(I32), d_scales[0].bitcast(I32).unsqueeze(1).to_broadcast([16, 8, G // 4]))
+        nc.scalar.dma_start(x_sc[:].bitcast(I32), x_scales[0].bitcast(I32).unsqueeze(1).to_broadcast([16, 8, T // 4]))
+        nc.scalar.dma_start(gain_raw[:], gn.rearrange("(p t) o -> p (t o)", t=PACK))
+        gain = keep.tile([P, PACK], F32, name="gain")
+        nc.scalar.activation(gain[:], gain_raw[:], COPY, scale=0.0625)
+
+        mem_rows = mem.rearrange("(p t) w -> t p w", t=PACK)
+        out_rows = out_0.rearrange("(p t) w -> t p w", t=PACK)
+        page = [keep.tile([P, U], F32, name=f"page{t}") for t in range(PACK)]
+        d_w = keep.tile([P, G], U32, name="d_w")
+        x_w = keep.tile([P, T], U32, name="x_w")
+
+        k1_t = load_list("k1_t", k1)
+        offs_t = load_list("offs_t", offs)
+        n5_t = load_list("n5_t", n5)
+        nc.sync.dma_start(page[0][:], mem_rows[0])
+        nc.sync.dma_start(d_w[:].bitcast(I32), words_of(d_words))
+        nc.sync.dma_start(page[1][:], mem_rows[1])
+        nc.sync.dma_start(x_w[:].bitcast(I32), words_of(x_words))
+        nc.sync.dma_start(page[2][:], mem_rows[2])
+        n1_t = load_list("n1_t", n1)
+        n2_t = load_list("n2_t", n2)
+        k2_t = load_list("k2_t", k2)
+        two_t = load_list("two_t", two)
+        nc.sync.dma_start(page[3][:], mem_rows[3])
+        n3_t = load_list("n3_t", n3)
+        n4_t = load_list("n4_t", n4)
+
+        planes = [keep.tile([P, 2 * S], U8, name=f"planes{s}", align_bytes=64) for s in range(2)]
+        w_sc_raw = keep.tile([P, N], U8, name="w_sc_raw")
+        for tile in planes + [w_sc_raw]:
+            nc.gpsimd.memset(tile[:].bitcast(I32), 0)
+
+        w_raw = keep.tile([P, N], U32, name="w_raw")
+        nc.sync.dma_start(w_raw[:].bitcast(I32), words_of(w1_words))
+        for q in range(4):
+            nc.sync.dma_start(w_sc_raw[32 * q : 32 * q + 4, :].bitcast(I32), w1_scales[0, 4 * q : 4 * q + 4, :].bitcast(I32))
+
+        old = [keep.tile([P, S], F32, name=f"old{t}") for t in range(PACK)]
+        for t in range(PACK):
+            nc.scalar.activation(old[t][:], page[t][:].indirect(n5_t[:]), COPY)
+
+        def deal(dst, src):
+            nc.vector.tensor_copy(dst.rearrange("p (t m) -> p t m", t=PACK), src.rearrange("p (m t) -> p t m", t=PACK))
+
+        def coded_layer(s, codes, tokens, move_queue):
+            d_bytes = keep.tile([P, H], U8, name=f"d_bytes{s}")
+            x_bytes = keep.tile([P, S], U8, name=f"x_bytes{s}")
+            both = keep.tile([P, 2 * S], U8, name=f"both{s}")
+            nc.vector.tensor_copy(d_bytes[:], d_sc[:].indirect(codes[:]))
+            nc.vector.tensor_copy(x_bytes[:], x_sc[:].indirect(tokens[:]))
+            deal(both[:, 0:H], d_bytes[:])
+            nc.vector.tensor_copy(both[:, H : H + S].bitcast(I32), x_bytes[:].bitcast(I32))
+            for c in range(4):
+                move_queue.dma_start(planes[s][c:P:32, :].bitcast(I32), both[8 * c : P : 32, :].bitcast(I32))
+            d_picked = keep.tile([P, H], U32, name=f"d_picked{s}")
+            d_dealt = keep.tile([P, H], U32, name=f"d_dealt{s}", align_bytes=64)
+            x_picked = keep.tile([P, S], U32, name=f"x_picked{s}", align_bytes=64)
+            nc.vector.tensor_copy(d_picked[:], d_w[:].indirect(codes[:]))
+            nc.vector.tensor_copy(x_picked[:], x_w[:].indirect(tokens[:]))
+            deal(d_dealt[:], d_picked[:])
+            rows = []
+            for t in range(PACK):
+                bank = psum.tile([P, S], F32, name=f"bank{PACK * s + t}")
+                cols = slice(P * t, P * (t + 1))
+                nc.tensor.matmul_mx(
+                    out=bank[:], lhsT=d_dealt[:, cols].bitcast(FP8X4), lhsT_scale=planes[s][:, cols],
+                    rhs=x_picked[:].bitcast(FP8X4), rhs_scale=planes[s][:, H : H + S], start=True, stop=True,
+                )
+                row = keep.tile([P, S], F32, name=f"rows{s}_{t}")
+                nc.vector.tensor_copy(row[:], bank[:])
+                rows.append(row)
+            return rows
+
+        def fetch_pair(dst, rows, first, second, h):
+            cols = slice(HALF_COLS * h, HALF_COLS * (h + 1))
+            nc.scalar.activation(dst[:, 0, :], rows[:].indirect(first[:, cols]), COPY)
+            nc.scalar.activation(dst[:, 1, :], rows[:].indirect(second[:, cols]), COPY)
+
+        a_rows = coded_layer(0, k1_t, offs_t, nc.scalar)
+        a_got = {}
+        for h in range(2):
+            for t in range(PACK):
+                a_got[h, t] = keep.tile([P, 2, HALF], F32, name=f"a_got{h}_{t}")
+                fetch_pair(a_got[h, t], a_rows[t], n1_t, n2_t, h)
+        b_rows = coded_layer(1, k2_t, two_t, nc.sync)
+
+        w_dealt = keep.tile([P, N], U32, name="w_dealt", align_bytes=64)
+        w_sc = keep.tile([P, N], U8, name="w_sc", align_bytes=64)
+        deal(w_dealt[:], w_raw[:])
+        deal(w_sc[:], w_sc_raw[:])
+
+        new = {}
+        for h in range(2):
+            larger = keep.tile([P, PACK, HALF], F32, name=f"larger{h}")
+            for t in range(PACK):
+                b_got = ring.tile([P, 2, HALF], F32, name="b_got")
+                fetch_pair(b_got, b_rows[t], n3_t, n4_t, h)
+                sums = ring.tile([P, 2, HALF], F32, name="sums")
+                nc.vector.tensor_tensor(sums[:], a_got[h, t][:], b_got[:], ADD)
+                nc.vector.tensor_tensor(larger[:, t, :], sums[:, 0, :], sums[:, 1, :], MAX)
+            z = keep.tile([P, HALF, PACK], BF16, name=f"z{h}", align_bytes=64)
+            nc.vector.tensor_tensor(
+                z[:].rearrange("p (c i) t -> p c t i", i=4),
+                larger[:].rearrange("p t (c i) -> p c t i", i=4),
+                gain[:].unsqueeze(1).unsqueeze(3).to_broadcast([P, HALF // 4, PACK, 4]),
+                MULT,
+            )
+            z_words = keep.tile([P, HALF], U32, name=f"z_words{h}", align_bytes=64)
+            z_sc = keep.tile([P, HALF], U8, name=f"z_sc{h}", align_bytes=64)
+            nc.vector.quantize_mx(out=z_words[:].bitcast(FP8X4), scales=z_sc[:], in_=z[:].rearrange("p c t -> p (c t)"))
+            for t in range(PACK):
+                bank = psum.tile([P, S], F32, name=f"bank{PACK * h + t}")
+                cols = slice(P * t, P * (t + 1))
+                nc.tensor.matmul_mx(
+                    out=bank[:, 0:HALF], lhsT=w_dealt[:, cols].bitcast(FP8X4), lhsT_scale=w_sc[:, cols],
+                    rhs=z_words[:].bitcast(FP8X4), rhs_scale=z_sc[:], start=True, stop=True,
+                )
+                new[h, t] = keep.tile([P, HALF], F32, name=f"new{h}_{t}")
+                nc.vector.scalar_tensor_tensor(
+                    new[h, t][:], old[t][:, HALF * h : HALF * (h + 1)], 0.5, bank[:, 0:HALF], MULT, MAX,
+                )
+
+        rounded = [keep.tile([P, OUT_W, PACK], BF16, name=f"rounded{c}", align_bytes=64) for c in range(OUT_PARTS)]
+        for h in range(2):
+            for t in range(PACK):
+                nc.scalar.activation(
+                    page[t][:].indirect(n5_t[:, HALF_COLS * h : HALF_COLS * (h + 1)]), new[h, t][:], COPY,
+                )
+                if h == 1:
+                    nc.sync.dma_start(out_rows[t], page[t][:])
+                    for c in range(OUT_PARTS):
+                        nc.vector.tensor_copy(rounded[c][:, :, t], page[t][:, OUT_W * c : OUT_W * (c + 1)])
+
+        out_sc = keep.tile([P, U], U8, name="out_sc", align_bytes=64)
+        for c in range(OUT_PARTS):
+            cols = slice(OUT_W * c, OUT_W * (c + 1))
+            out_words = keep.tile([P, OUT_W], U32, name=f"out_words{c}", align_bytes=64)
+            nc.vector.quantize_mx(
+                out=out_words[:].bitcast(FP8X4), scales=out_sc[:, cols], in_=rounded[c][:].rearrange("p c t -> p (c t)"),
+            )
+            nc.sync.dma_start(words_of(out_1)[:, cols], out_words[:].bitcast(I32))
+        for q in range(4):
+            nc.scalar.dma_start(out_2[0, 4 * q : 4 * q + 4, :].bitcast(I32), out_sc[32 * q : 32 * q + 4, :].bitcast(I32))

@@ -20,7 +20,7 @@ COPY = mybir.ActivationFunctionType.Copy
 P = 128
 PACK = 4
 HALF = S // 2
-HALF_COLS = HALF // 16
+WHOLE = 3
 OUT_PARTS = 4
 OUT_W = U // OUT_PARTS
 
@@ -44,9 +44,9 @@ def tile_picked_twpqpathbpagex_none_po_kernel(
             nc.sync.dma_start(tile[:], dram)
             return tile
 
+        gain_raw = keep.tile([P, PACK], F32, name="gain_raw")
         d_sc = keep.tile([P, G], U8, name="d_sc")
         x_sc = keep.tile([P, T], U8, name="x_sc")
-        gain_raw = keep.tile([P, PACK], F32, name="gain_raw")
         nc.scalar.dma_start(d_sc[:].bitcast(I32), d_scales[0].bitcast(I32).unsqueeze(1).to_broadcast([16, 8, G // 4]))
         nc.scalar.dma_start(x_sc[:].bitcast(I32), x_scales[0].bitcast(I32).unsqueeze(1).to_broadcast([16, 8, T // 4]))
         nc.scalar.dma_start(gain_raw[:], gn.rearrange("(p t) o -> p (t o)", t=PACK))
@@ -55,60 +55,60 @@ def tile_picked_twpqpathbpagex_none_po_kernel(
 
         mem_rows = mem.rearrange("(p t) w -> t p w", t=PACK)
         out_rows = out_0.rearrange("(p t) w -> t p w", t=PACK)
-        page = [keep.tile([P, U], F32, name=f"page{t}") for t in range(PACK)]
+        page = []
+
+        def load_page(tile):
+            nc.sync.dma_start(tile[:], mem_rows[len(page)])
+            page.append(tile)
+
         d_w = keep.tile([P, G], U32, name="d_w")
         x_w = keep.tile([P, T], U32, name="x_w")
-
         k1_t = load_list("k1_t", k1)
         offs_t = load_list("offs_t", offs)
         n5_t = load_list("n5_t", n5)
-        nc.sync.dma_start(page[0][:], mem_rows[0])
+        load_page(keep.tile([P, U], F32, name="page0"))
         nc.sync.dma_start(d_w[:].bitcast(I32), words_of(d_words))
-        nc.sync.dma_start(page[1][:], mem_rows[1])
+        load_page(keep.tile([P, U], F32, name="page1"))
         nc.sync.dma_start(x_w[:].bitcast(I32), words_of(x_words))
-        nc.sync.dma_start(page[2][:], mem_rows[2])
+        load_page(keep.tile([P, U], F32, name="page2"))
         n1_t = load_list("n1_t", n1)
         n2_t = load_list("n2_t", n2)
         k2_t = load_list("k2_t", k2)
         two_t = load_list("two_t", two)
-        nc.sync.dma_start(page[3][:], mem_rows[3])
+        load_page(keep.tile([P, U], F32, name="page3"))
         n3_t = load_list("n3_t", n3)
         n4_t = load_list("n4_t", n4)
+        w_raw = keep.tile([P, N], U32, name="w_raw")
+        nc.sync.dma_start(w_raw[:].bitcast(I32), words_of(w1_words))
 
-        planes = [keep.tile([P, 2 * S], U8, name=f"planes{s}", align_bytes=64) for s in range(2)]
+        planes = [keep.tile([P, H + S], U8, name=f"planes{s}", tag=f"planes{s}", align_bytes=64) for s in range(2)]
         w_sc_raw = keep.tile([P, N], U8, name="w_sc_raw")
         for tile in planes + [w_sc_raw]:
             nc.gpsimd.memset(tile[:].bitcast(I32), 0)
-
-        w_raw = keep.tile([P, N], U32, name="w_raw")
-        nc.sync.dma_start(w_raw[:].bitcast(I32), words_of(w1_words))
         for q in range(4):
-            nc.sync.dma_start(w_sc_raw[32 * q : 32 * q + 4, :].bitcast(I32), w1_scales[0, 4 * q : 4 * q + 4, :].bitcast(I32))
-
-        old = [keep.tile([P, S], F32, name=f"old{t}") for t in range(PACK)]
-        for t in range(PACK):
-            nc.scalar.activation(old[t][:], page[t][:].indirect(n5_t[:]), COPY)
+            nc.gpsimd.dma_start(w_sc_raw[32 * q : 32 * q + 4, :].bitcast(I32), w1_scales[0, 4 * q : 4 * q + 4, :].bitcast(I32))
 
         def deal(dst, src):
             nc.vector.tensor_copy(dst.rearrange("p (t m) -> p t m", t=PACK), src.rearrange("p (m t) -> p t m", t=PACK))
 
-        def coded_layer(s, codes, tokens, move_queue):
-            d_bytes = keep.tile([P, H], U8, name=f"d_bytes{s}")
-            x_bytes = keep.tile([P, S], U8, name=f"x_bytes{s}")
-            both = keep.tile([P, 2 * S], U8, name=f"both{s}")
-            nc.vector.tensor_copy(d_bytes[:], d_sc[:].indirect(codes[:]))
-            nc.vector.tensor_copy(x_bytes[:], x_sc[:].indirect(tokens[:]))
-            deal(both[:, 0:H], d_bytes[:])
-            nc.vector.tensor_copy(both[:, H : H + S].bitcast(I32), x_bytes[:].bitcast(I32))
+        def pick(dst, table, entries):
+            nc.vector.tensor_copy(dst, table[:].indirect(entries[:]))
+
+        def place_scales(s, d_bytes, x_bytes):
+            both = keep.tile([P, H + S], U8, name=f"both{s}")
+            deal(both[:, 0:H], d_bytes)
+            nc.vector.tensor_copy(both[:, H : H + S].bitcast(I32), x_bytes.bitcast(I32))
             for c in range(4):
-                move_queue.dma_start(planes[s][c:P:32, :].bitcast(I32), both[8 * c : P : 32, :].bitcast(I32))
-            d_picked = keep.tile([P, H], U32, name=f"d_picked{s}")
-            d_dealt = keep.tile([P, H], U32, name=f"d_dealt{s}", align_bytes=64)
-            x_picked = keep.tile([P, S], U32, name=f"x_picked{s}", align_bytes=64)
-            nc.vector.tensor_copy(d_picked[:], d_w[:].indirect(codes[:]))
-            nc.vector.tensor_copy(x_picked[:], x_w[:].indirect(tokens[:]))
+                (nc.scalar, nc.sync)[s].dma_start(planes[s][c:P:32, :].bitcast(I32), both[8 * c : P : 32, :].bitcast(I32))
+
+        def coded_product(s, codes, tokens, tags):
+            d_picked = keep.tile([P, H], U32, name=f"d_picked{s}", tag=tags[0], align_bytes=64)
+            pick(d_picked[:], d_w, codes)
+            d_dealt = keep.tile([P, H], U32, name=f"d_dealt{s}", tag=tags[1], align_bytes=64)
             deal(d_dealt[:], d_picked[:])
-            rows = []
+            x_picked = keep.tile([P, S], U32, name=f"x_picked{s}", tag=tags[2], align_bytes=64)
+            pick(x_picked[:], x_w, tokens)
+            banks = []
             for t in range(PACK):
                 bank = psum.tile([P, S], F32, name=f"bank{PACK * s + t}")
                 cols = slice(P * t, P * (t + 1))
@@ -116,37 +116,66 @@ def tile_picked_twpqpathbpagex_none_po_kernel(
                     out=bank[:], lhsT=d_dealt[:, cols].bitcast(FP8X4), lhsT_scale=planes[s][:, cols],
                     rhs=x_picked[:].bitcast(FP8X4), rhs_scale=planes[s][:, H : H + S], start=True, stop=True,
                 )
-                row = keep.tile([P, S], F32, name=f"rows{s}_{t}")
-                nc.vector.tensor_copy(row[:], bank[:])
-                rows.append(row)
-            return rows
+                banks.append(bank)
+            return banks
 
-        def fetch_pair(dst, rows, first, second, h):
-            cols = slice(HALF_COLS * h, HALF_COLS * (h + 1))
-            nc.scalar.activation(dst[:, 0, :], rows[:].indirect(first[:, cols]), COPY)
-            nc.scalar.activation(dst[:, 1, :], rows[:].indirect(second[:, cols]), COPY)
+        def fetch_pair(name, rows, first, second, start, width):
+            got = keep.tile([P, 2, width], F32, name=name)
+            entries = slice(start // 16, (start + width) // 16)
+            nc.scalar.activation(got[:, 0, :], rows[:].indirect(first[:, entries]), COPY)
+            nc.scalar.activation(got[:, 1, :], rows[:].indirect(second[:, entries]), COPY)
+            return got
 
-        a_rows = coded_layer(0, k1_t, offs_t, nc.scalar)
-        a_got = {}
-        for h in range(2):
-            for t in range(PACK):
-                a_got[h, t] = keep.tile([P, 2, HALF], F32, name=f"a_got{h}_{t}")
-                fetch_pair(a_got[h, t], a_rows[t], n1_t, n2_t, h)
-        b_rows = coded_layer(1, k2_t, two_t, nc.sync)
+        bytes_a = keep.tile([P, H + S], U8, name="bytes_a")
+        pick(bytes_a[:, 0:H], d_sc, k1_t)
+        pick(bytes_a[:, H : H + S], x_sc, offs_t)
+        place_scales(0, bytes_a[:, 0:H], bytes_a[:, H : H + S])
 
-        w_dealt = keep.tile([P, N], U32, name="w_dealt", align_bytes=64)
-        w_sc = keep.tile([P, N], U8, name="w_sc", align_bytes=64)
+        a_old = [keep.tile([P, 2 * S], F32, name=f"a_old{t}") for t in range(PACK)]
+        for t in range(PACK):
+            nc.scalar.activation(a_old[t][:, S : 2 * S], page[t][:].indirect(n5_t[:]), COPY)
+
+        a_banks = coded_product(0, k1_t, offs_t, ("slot_d", "slot_b", "slot_a"))
+        bytes_b = keep.tile([P, H + S], U8, name="bytes_b", tag="slot_d", align_bytes=64)
+        pick(bytes_b[:, 0:H], d_sc, k2_t)
+        a_got = []
+        for t in range(PACK):
+            nc.vector.tensor_copy(a_old[t][:, 0:S], a_banks[t][:])
+            if t == 0:
+                pick(bytes_b[:, H : H + S], x_sc, two_t)
+            if t == 1:
+                place_scales(1, bytes_b[:, 0:H], bytes_b[:, H : H + S])
+            width = S if t < WHOLE else HALF
+            a_got.append(fetch_pair(f"a_got{t}", a_old[t], n1_t, n2_t, 0, width))
+
+        b_banks = coded_product(1, k2_t, two_t, ("slot_b", "slot_c", "slot_a"))
+        w_dealt = keep.tile([P, N], U32, name="w_dealt", tag="slot_b", align_bytes=64)
+        w_sc = keep.tile([P, N], U8, name="w_sc", tag="planes0", align_bytes=64)
+        b_rows = []
+        for t in range(PACK):
+            row = keep.tile([P, S], F32, name=f"b_rows{t}")
+            nc.vector.tensor_copy(row[:], b_banks[t][:])
+            b_rows.append(row)
         deal(w_dealt[:], w_raw[:])
         deal(w_sc[:], w_sc_raw[:])
 
-        new = {}
+        new = [keep.tile([P, S], F32, name=f"new{t}") for t in range(PACK)]
         for h in range(2):
+            half = slice(HALF * h, HALF * (h + 1))
             larger = keep.tile([P, PACK, HALF], F32, name=f"larger{h}")
             for t in range(PACK):
-                b_got = ring.tile([P, 2, HALF], F32, name="b_got")
-                fetch_pair(b_got, b_rows[t], n3_t, n4_t, h)
-                sums = ring.tile([P, 2, HALF], F32, name="sums")
-                nc.vector.tensor_tensor(sums[:], a_got[h, t][:], b_got[:], ADD)
+                if t < WHOLE:
+                    a_half = a_got[t][:, :, half]
+                elif h == 0:
+                    a_half = a_got[t][:]
+                else:
+                    a_half = fetch_pair(f"a_got{t}", a_old[t], n1_t, n2_t, HALF, HALF)[:]
+                b_got = fetch_pair(f"b_got{t}", b_rows[t], n3_t, n4_t, HALF * h, HALF)
+                if h == 1 and t >= 2:
+                    sums = keep.tile([P, 2, HALF], F32, name="late_sums", tag=("z_sc0", "z_words0")[t % 2], align_bytes=64)
+                else:
+                    sums = ring.tile([P, 2, HALF], F32, name="sums")
+                nc.vector.tensor_tensor(sums[:], a_half, b_got[:], ADD)
                 nc.vector.tensor_tensor(larger[:, t, :], sums[:, 0, :], sums[:, 1, :], MAX)
             z = keep.tile([P, HALF, PACK], BF16, name=f"z{h}", align_bytes=64)
             nc.vector.tensor_tensor(
@@ -155,8 +184,8 @@ def tile_picked_twpqpathbpagex_none_po_kernel(
                 gain[:].unsqueeze(1).unsqueeze(3).to_broadcast([P, HALF // 4, PACK, 4]),
                 MULT,
             )
-            z_words = keep.tile([P, HALF], U32, name=f"z_words{h}", align_bytes=64)
-            z_sc = keep.tile([P, HALF], U8, name=f"z_sc{h}", align_bytes=64)
+            z_words = keep.tile([P, HALF], U32, name=f"z_words{h}", tag=f"z_words{h}", align_bytes=64)
+            z_sc = keep.tile([P, HALF], U8, name=f"z_sc{h}", tag=f"z_sc{h}", align_bytes=64)
             nc.vector.quantize_mx(out=z_words[:].bitcast(FP8X4), scales=z_sc[:], in_=z[:].rearrange("p c t -> p (c t)"))
             for t in range(PACK):
                 bank = psum.tile([P, S], F32, name=f"bank{PACK * h + t}")
@@ -165,17 +194,16 @@ def tile_picked_twpqpathbpagex_none_po_kernel(
                     out=bank[:, 0:HALF], lhsT=w_dealt[:, cols].bitcast(FP8X4), lhsT_scale=w_sc[:, cols],
                     rhs=z_words[:].bitcast(FP8X4), rhs_scale=z_sc[:], start=True, stop=True,
                 )
-                new[h, t] = keep.tile([P, HALF], F32, name=f"new{h}_{t}")
                 nc.vector.scalar_tensor_tensor(
-                    new[h, t][:], old[t][:, HALF * h : HALF * (h + 1)], 0.5, bank[:, 0:HALF], MULT, MAX,
+                    new[t][:, half], a_old[t][:, S + HALF * h : S + HALF * (h + 1)], 0.5, bank[:, 0:HALF], MULT, MAX,
                 )
 
         rounded = [keep.tile([P, OUT_W, PACK], BF16, name=f"rounded{c}", align_bytes=64) for c in range(OUT_PARTS)]
         for h in range(2):
             for t in range(PACK):
-                nc.scalar.activation(
-                    page[t][:].indirect(n5_t[:, HALF_COLS * h : HALF_COLS * (h + 1)]), new[h, t][:], COPY,
-                )
+                cut = HALF if t < PACK - 1 else HALF // 2
+                lo, hi = (0, cut) if h == 0 else (cut, S)
+                nc.scalar.activation(page[t][:].indirect(n5_t[:, lo // 16 : hi // 16]), new[t][:, lo:hi], COPY)
                 if h == 1:
                     nc.sync.dma_start(out_rows[t], page[t][:])
                     for c in range(OUT_PARTS):
@@ -190,4 +218,4 @@ def tile_picked_twpqpathbpagex_none_po_kernel(
             )
             nc.sync.dma_start(words_of(out_1)[:, cols], out_words[:].bitcast(I32))
         for q in range(4):
-            nc.scalar.dma_start(out_2[0, 4 * q : 4 * q + 4, :].bitcast(I32), out_sc[32 * q : 32 * q + 4, :].bitcast(I32))
+            (nc.scalar if q < 3 else nc.sync).dma_start(out_2[0, 4 * q : 4 * q + 4, :].bitcast(I32), out_sc[32 * q : 32 * q + 4, :].bitcast(I32))

@@ -210,12 +210,14 @@ def tile_picked_twpqpathbpagex_none_po_kernel(
                         nc.vector.tensor_copy(rounded[c][:, :, t], page[t][:, OUT_W * c : OUT_W * (c + 1)])
 
         out_sc = keep.tile([P, U], U8, name="out_sc", align_bytes=64)
+        out_words = keep.tile([P, U], U32, name="out_words", align_bytes=64)
         for c in range(OUT_PARTS):
             cols = slice(OUT_W * c, OUT_W * (c + 1))
-            out_words = keep.tile([P, OUT_W], U32, name=f"out_words{c}", align_bytes=64)
             nc.vector.quantize_mx(
-                out=out_words[:].bitcast(FP8X4), scales=out_sc[:, cols], in_=rounded[c][:].rearrange("p c t -> p (c t)"),
+                out=out_words[:, cols].bitcast(FP8X4), scales=out_sc[:, cols], in_=rounded[c][:].rearrange("p c t -> p (c t)"),
             )
-            nc.sync.dma_start(words_of(out_1)[:, cols], out_words[:].bitcast(I32))
+            if c % 2 == 1:
+                done = slice(OUT_W * (c - 1), OUT_W * (c + 1))
+                nc.sync.dma_start(words_of(out_1)[:, done], out_words[:, done].bitcast(I32))
         for q in range(4):
             (nc.scalar if q < 3 else nc.sync).dma_start(out_2[0, 4 * q : 4 * q + 4, :].bitcast(I32), out_sc[32 * q : 32 * q + 4, :].bitcast(I32))

from contextlib import ExitStack

import concourse.mybir as mybir

K, T, S, N, G, H, U = 512, 1024, 512, 512, 2048, 512, 1024
FLOPS = 2 * K * H * S * 2 + 2 * H * N * S

F32 = mybir.dt.float32
BF16 = mybir.dt.bfloat16
I32 = mybir.dt.int32
U32 = mybir.dt.uint32
U16 = mybir.dt.uint16
U8 = mybir.dt.uint8
FP8X4 = mybir.dt.float8_e4m3fn_x4
ADD = mybir.AluOpType.add
MULT = mybir.AluOpType.mult
MAX = mybir.AluOpType.max
COPY = mybir.ActivationFunctionType.Copy

P = 128
PACK = 4
HALF = S // 2
WHOLE = 3
OUT_PARTS = 4
OUT_W = U // OUT_PARTS


def words_of(dram):
    return dram[0].rearrange("p n t -> p (n t)").bitcast(I32)


def tile_picked_twpqpathbpagex_none_po_kernel(
    tc, x_words, x_scales, d_words, d_scales, gn, w1_words, w1_scales, mem,
    offs, k1, two, k2, n1, n2, n3, n4, n5, out_0, out_1, out_2,
):
    nc = tc.nc
    with ExitStack() as ctx:
        keep = ctx.enter_context(tc.tile_pool(name="keep", bufs=1))
        ring = ctx.enter_context(tc.tile_pool(name="ring", bufs=3))
        psum = ctx.enter_context(tc.psum_pool(name="psum", bufs=1))

        def load_list(name, dram):
            tile = keep.tile([P, S // 16], U16, name=name)
            nc.sync.dma_start(tile[:], dram)
            return tile

        gain_raw = keep.tile([P, PACK], F32, name="gain_raw")
        d_sc = keep.tile([P, G], U8, name="d_sc")
        x_sc = keep.tile([P, T], U8, name="x_sc")
        nc.scalar.dma_start(d_sc[:].bitcast(I32), d_scales[0].bitcast(I32).unsqueeze(1).to_broadcast([16, 8, G // 4]))
        nc.scalar.dma_start(x_sc[:].bitcast(I32), x_scales[0].bitcast(I32).unsqueeze(1).to_broadcast([16, 8, T // 4]))
        nc.scalar.dma_start(gain_raw[:], gn.rearrange("(p t) o -> p (t o)", t=PACK))
        gain = keep.tile([P, PACK], F32, name="gain")
        nc.scalar.activation(gain[:], gain_raw[:], COPY, scale=0.0625)

        mem_rows = mem.rearrange("(p t) w -> t p w", t=PACK)
        out_rows = out_0.rearrange("(p t) w -> t p w", t=PACK)
        page = []

        def load_page(tile):
            nc.sync.dma_start(tile[:], mem_rows[len(page)])
            page.append(tile)

        d_w = keep.tile([P, G], U32, name="d_w")
        x_w = keep.tile([P, T], U32, name="x_w")
        k1_t = load_list("k1_t", k1)
        offs_t = load_list("offs_t", offs)
        n5_t = load_list("n5_t", n5)
        load_page(keep.tile([P, U], F32, name="page0"))
        nc.sync.dma_start(d_w[:].bitcast(I32), words_of(d_words))
        load_page(keep.tile([P, U], F32, name="page1"))
        nc.sync.dma_start(x_w[:].bitcast(I32), words_of(x_words))
        load_page(keep.tile([P, U], F32, name="page2"))
        n1_t = load_list("n1_t", n1)
        n2_t = load_list("n2_t", n2)
        k2_t = load_list("k2_t", k2)
        two_t = load_list("two_t", two)
        load_page(keep.tile([P, U], F32, name="page3"))
        n3_t = load_list("n3_t", n3)
        n4_t = load_list("n4_t", n4)
        w_raw = keep.tile([P, N], U32, name="w_raw")
        nc.sync.dma_start(w_raw[:].bitcast(I32), words_of(w1_words))

        planes = [keep.tile([P, H + S], U8, name=f"planes{s}", tag=f"planes{s}", align_bytes=64) for s in range(2)]
        w_sc_raw = keep.tile([P, N], U8, name="w_sc_raw")
        for tile in planes + [w_sc_raw]:
            nc.gpsimd.memset(tile[:].bitcast(I32), 0)
        for q in range(4):
            nc.gpsimd.dma_start(w_sc_raw[32 * q : 32 * q + 4, :].bitcast(I32), w1_scales[0, 4 * q : 4 * q + 4, :].bitcast(I32))

        def deal(dst, src):
            nc.vector.tensor_copy(dst.rearrange("p (t m) -> p t m", t=PACK), src.rearrange("p (m t) -> p t m", t=PACK))

        def pick(dst, table, entries):
            nc.vector.tensor_copy(dst, table[:].indirect(entries[:]))

        def place_scales(s, d_bytes, x_bytes):
            both = keep.tile([P, H + S], U8, name=f"both{s}")
            deal(both[:, 0:H], d_bytes)
            nc.vector.tensor_copy(both[:, H : H + S].bitcast(I32), x_bytes.bitcast(I32))
            for c in range(4):
                (nc.scalar, nc.sync)[s].dma_start(planes[s][c:P:32, :].bitcast(I32), both[8 * c : P : 32, :].bitcast(I32))

        def coded_product(s, codes, tokens, tags):
            d_picked = keep.tile([P, H], U32, name=f"d_picked{s}", tag=tags[0], align_bytes=64)
            pick(d_picked[:], d_w, codes)
            d_dealt = keep.tile([P, H], U32, name=f"d_dealt{s}", tag=tags[1], align_bytes=64)
            deal(d_dealt[:], d_picked[:])
            x_picked = keep.tile([P, S], U32, name=f"x_picked{s}", tag=tags[2], align_bytes=64)
            pick(x_picked[:], x_w, tokens)
            banks = []
            for t in range(PACK):
                bank = psum.tile([P, S], F32, name=f"bank{PACK * s + t}")
                cols = slice(P * t, P * (t + 1))
                nc.tensor.matmul_mx(
                    out=bank[:], lhsT=d_dealt[:, cols].bitcast(FP8X4), lhsT_scale=planes[s][:, cols],
                    rhs=x_picked[:].bitcast(FP8X4), rhs_scale=planes[s][:, H : H + S], start=True, stop=True,
                )
                banks.append(bank)
            return banks

        def fetch_pair(name, rows, first, second, start, width):
            got = keep.tile([P, 2, width], F32, name=name)
            entries = slice(start // 16, (start + width) // 16)
            nc.scalar.activation(got[:, 0, :], rows[:].indirect(first[:, entries]), COPY)
            nc.scalar.activation(got[:, 1, :], rows[:].indirect(second[:, entries]), COPY)
            return got

        bytes_a = keep.tile([P, H + S], U8, name="bytes_a")
        pick(bytes_a[:, 0:H], d_sc, k1_t)
        pick(bytes_a[:, H : H + S], x_sc, offs_t)
        place_scales(0, bytes_a[:, 0:H], bytes_a[:, H : H + S])

        a_old = [keep.tile([P, 2 * S], F32, name=f"a_old{t}") for t in range(PACK)]
        for t in range(PACK):
            nc.scalar.activation(a_old[t][:, S : 2 * S], page[t][:].indirect(n5_t[:]), COPY)

        a_banks = coded_product(0, k1_t, offs_t, ("slot_d", "slot_b", "slot_a"))
        bytes_b = keep.tile([P, H + S], U8, name="bytes_b", tag="slot_d", align_bytes=64)
        pick(bytes_b[:, 0:H], d_sc, k2_t)
        a_got = []
        for t in range(PACK):
            nc.vector.tensor_copy(a_old[t][:, 0:S], a_banks[t][:])
            if t == 0:
                pick(bytes_b[:, H : H + S], x_sc, two_t)
            if t == 1:
                place_scales(1, bytes_b[:, 0:H], bytes_b[:, H : H + S])
            width = S if t < WHOLE else HALF
            a_got.append(fetch_pair(f"a_got{t}", a_old[t], n1_t, n2_t, 0, width))

        b_banks = coded_product(1, k2_t, two_t, ("slot_b", "slot_c", "slot_a"))
        w_dealt = keep.tile([P, N], U32, name="w_dealt", tag="slot_b", align_bytes=64)
        w_sc = keep.tile([P, N], U8, name="w_sc", tag="planes0", align_bytes=64)
        b_rows = []
        for t in range(PACK):
            row = keep.tile([P, S], F32, name=f"b_rows{t}")
            nc.vector.tensor_copy(row[:], b_banks[t][:])
            b_rows.append(row)
        deal(w_dealt[:], w_raw[:])
        deal(w_sc[:], w_sc_raw[:])

        new = [keep.tile([P, S], F32, name=f"new{t}") for t in range(PACK)]
        for h in range(2):
            half = slice(HALF * h, HALF * (h + 1))
            larger = keep.tile([P, PACK, HALF], F32, name=f"larger{h}")
            for t in range(PACK):
                if t < WHOLE:
                    a_half = a_got[t][:, :, half]
                elif h == 0:
                    a_half = a_got[t][:]
                else:
                    a_half = fetch_pair(f"a_got{t}", a_old[t], n1_t, n2_t, HALF, HALF)[:]
                b_got = fetch_pair(f"b_got{t}", b_rows[t], n3_t, n4_t, HALF * h, HALF)
                if h == 1 and t >= 2:
                    sums = keep.tile([P, 2, HALF], F32, name="late_sums", tag=("z_sc0", "z_words0")[t % 2], align_bytes=64)
                else:
                    sums = ring.tile([P, 2, HALF], F32, name="sums")
                nc.vector.tensor_tensor(sums[:], a_half, b_got[:], ADD)
                nc.vector.tensor_tensor(larger[:, t, :], sums[:, 0, :], sums[:, 1, :], MAX)
            z = keep.tile([P, HALF, PACK], BF16, name=f"z{h}", align_bytes=64)
            nc.vector.tensor_tensor(
                z[:].rearrange("p (c i) t -> p c t i", i=4),
                larger[:].rearrange("p t (c i) -> p c t i", i=4),
                gain[:].unsqueeze(1).unsqueeze(3).to_broadcast([P, HALF // 4, PACK, 4]),
                MULT,
            )
            z_words = keep.tile([P, HALF], U32, name=f"z_words{h}", tag=f"z_words{h}", align_bytes=64)
            z_sc = keep.tile([P, HALF], U8, name=f"z_sc{h}", tag=f"z_sc{h}", align_bytes=64)
            nc.vector.quantize_mx(out=z_words[:].bitcast(FP8X4), scales=z_sc[:], in_=z[:].rearrange("p c t -> p (c t)"))
            for t in range(PACK):
                bank = psum.tile([P, S], F32, name=f"bank{PACK * h + t}")
                cols = slice(P * t, P * (t + 1))
                nc.tensor.matmul_mx(
                    out=bank[:, 0:HALF], lhsT=w_dealt[:, cols].bitcast(FP8X4), lhsT_scale=w_sc[:, cols],
                    rhs=z_words[:].bitcast(FP8X4), rhs_scale=z_sc[:], start=True, stop=True,
                )
                nc.vector.scalar_tensor_tensor(
                    new[t][:, half], a_old[t][:, S + HALF * h : S + HALF * (h + 1)], 0.5, bank[:, 0:HALF], MULT, MAX,
                )

        rounded = [keep.tile([P, OUT_W, PACK], BF16, name=f"rounded{c}", align_bytes=64) for c in range(OUT_PARTS)]
        for h in range(2):
            for t in range(PACK):
                cut = HALF if t < PACK - 1 else HALF // 2
                lo, hi = (0, cut) if h == 0 else (cut, S)
                nc.scalar.activation(page[t][:].indirect(n5_t[:, lo // 16 : hi // 16]), new[t][:, lo:hi], COPY)
                if h == 1:
                    nc.sync.dma_start(out_rows[t], page[t][:])
                    for c in range(OUT_PARTS):
                        nc.vector.tensor_copy(rounded[c][:, :, t], page[t][:, OUT_W * c : OUT_W * (c + 1)])

        out_sc = keep.tile([P, U], U8, name="out_sc", align_bytes=64)
        out_words = keep.tile([P, U], U32, name="out_words", align_bytes=64)
        for c in range(OUT_PARTS):
            cols = slice(OUT_W * c, OUT_W * (c + 1))
            nc.vector.quantize_mx(
                out=out_words[:, cols].bitcast(FP8X4), scales=out_sc[:, cols], in_=rounded[c][:].rearrange("p c t -> p (c t)"),
            )
            if c % 2 == 1:
                done = slice(OUT_W * (c - 1), OUT_W * (c + 1))
                nc.sync.dma_start(words_of(out_1)[:, done], out_words[:, done].bitcast(I32))
        for q in range(4):
            (nc.scalar if q < 3 else nc.sync).dma_start(out_2[0, 4 * q : 4 * q + 4, :].bitcast(I32), out_sc[32 * q : 32 * q + 4, :].bitcast(I32))
